import numpy as np
import ml_dtypes


def mxq(x, axis, fmt="e4m3"):
    dtype, down = {"e4m3": (ml_dtypes.float8_e4m3fn, 7), "e5m2": (ml_dtypes.float8_e5m2, 14)}[fmt]
    v = np.moveaxis(np.asarray(x, np.float32).astype(ml_dtypes.bfloat16).astype(np.float64), axis, -1)
    blocks = v.reshape(v.shape[:-1] + (-1, 32))
    amax = np.abs(blocks).max(-1, keepdims=True)
    byte = np.maximum(np.where(amax > 0, np.frexp(amax)[1] - 1 + 127, 0) - down, 1)
    scale = np.exp2(byte - 127.0)
    codes = (blocks / scale).astype(np.float32).astype(dtype).astype(np.float64)
    return np.moveaxis((codes * scale).reshape(v.shape), -1, axis)


WIDE = False


def mx_kscale(k):
    if not WIDE:
        return np.ones(k)
    levels = np.array([10, -10, 5, -5, 0])
    if k % 512:
        return np.exp2(np.random.permutation(np.resize(levels, k // 32))).repeat(32)
    a = np.empty((k // 512, 16))
    for p in range(k // 512):
        a[p, :8] = np.random.permutation(np.resize(levels, 8))
        for g in range(8):
            far = levels[np.abs(levels - a[p, g]) >= 10]
            a[p, g + 8] = far[np.random.randint(len(far))]
    return np.exp2(a.ravel()).repeat(32)


def f64(x):
    return np.asarray(x).astype(np.float64)


def striped(idx):
    return np.tile(np.asarray(idx).reshape(-1, 16).T, (8, 1)).astype(np.uint16)


def unstriped(offs):
    return offs[:16].T.reshape(-1).astype(np.int64)


E2M1 = np.array([0.0, 0.5, 1.0, 1.5, 2.0, 3.0, 4.0, 6.0, -0.0, -0.5, -1.0, -1.5, -2.0, -3.0, -4.0, -6.0])


def pack_weight(w, fmt):
    k, n = w.shape
    w = f64(np.asarray(w, np.float32).astype(ml_dtypes.bfloat16)).reshape(k // 32, 32, n)
    amax = np.abs(w).max(1)
    if fmt == "e4m3":
        byte = np.frexp(amax)[1] - 1 + 127 - 7
    else:
        mant, ex = np.frexp(amax / 6.0)
        byte = np.where(mant > 0.5, ex, ex - 1) + 127
    byte = np.clip(np.where(amax > 0, byte, 1), 1, 254)
    scaled = (w * np.exp2(127.0 - byte)[:, None, :]).reshape(k, n).astype(np.float32)
    by_word = np.ascontiguousarray(scaled.reshape(k // 512, 128, 4, n).transpose(0, 1, 3, 2))
    if fmt == "e4m3":
        words = by_word.astype(ml_dtypes.float8_e4m3fn).view(np.uint8)
    else:
        c = by_word.astype(ml_dtypes.float4_e2m1fn).view(np.uint8) & 0xF
        words = (c[..., 0::2] | (c[..., 1::2] << 4)).reshape(k // 512, 128, 2 * n)
    return np.ascontiguousarray(words), np.ascontiguousarray(byte.astype(np.uint8).reshape(k // 512, 16, n))


def unpack_weight(words, scales, fmt):
    g, _, n = scales.shape
    words = np.ascontiguousarray(words).reshape(g, 128, n, -1)
    if fmt == "e4m3":
        vals = words.view(ml_dtypes.float8_e4m3fn).astype(np.float64)
    else:
        nib = np.empty((g, 128, n, 4), np.uint8)
        nib[..., 0::2] = words & 0xF
        nib[..., 1::2] = words >> 4
        vals = E2M1[nib]
    vals = vals * np.repeat(np.exp2(scales.astype(np.float64) - 127.0), 8, axis=1)[..., None]
    return vals.transpose(0, 1, 3, 2).reshape(g * 512, n)


def sigmoid(v):
    return 1.0 / (1.0 + np.exp(-v))


D, T, I, Q, E, M = 512, 1024, 512, 512, 512, 1024


def setup_inputs():
    n = np.random.standard_normal
    idx = np.random.permutation(T)[:I]
    idx2 = np.random.permutation(T)[:I]
    idx3 = np.random.permutation(M)[:I]
    fd = mx_kscale(D)
    fq = mx_kscale(Q)
    keysp = pack_weight(n((D, T)) / fd[:, None], "e2m1")
    return {
        "query": (n((D, Q)) * 1.0 / np.sqrt(D) * fd[:, None]).astype(np.float32),
        "keys_words": keysp[0],
        "keys_scales": keysp[1],
        "qs": (np.random.uniform(0.5, 2.0, (Q, 1)) * fq[:, None]).astype(np.float32),
        "msgs": (n((Q, E)) * 1 / np.sqrt(Q) / fq[:, None]).astype(np.float32),
        "old": (n((E, M)) * 1.0).astype(np.float32),
        "fade": (np.random.uniform(0.3, 0.9, (1, M))).astype(np.float32),
        "offs": striped(idx),
        "offs2": striped(idx2),
        "offs3": striped(idx3),
    }


def reference(query, keys_words, keys_scales, qs, msgs, old, fade, offs, offs2, offs3):
    idx = unstriped(offs)
    idx2 = unstriped(offs2)
    idx3 = unstriped(offs3)
    keysu = unpack_weight(keys_words, keys_scales, "e2m1")
    queryq = mxq(f64(query), 0, "e4m3")
    a = queryq.T @ keysu
    s = a[:, idx] - a[:, idx2]
    w = sigmoid(s)
    wq = w * f64(qs)
    msgsq = mxq(f64(msgs), 0, "e4m3")
    wqq = mxq(wq, 0, "e4m3")
    dl = msgsq.T @ wqq
    df = np.zeros((E, M))
    df[:, idx3] = dl
    y = f64(old) * f64(fade) + df
    return y

from contextlib import ExitStack

import concourse.mybir as mybir
from concourse.masks import make_identity

F32 = mybir.dt.float32
BF16 = mybir.dt.bfloat16
I32 = mybir.dt.int32
U32 = mybir.dt.uint32
U16 = mybir.dt.uint16
U8 = mybir.dt.uint8
FP8X4 = mybir.dt.float8_e4m3fn_x4
FP4X4 = mybir.dt.float4_e2m1fn_x4
ALU = mybir.AluOpType
ACT = mybir.ActivationFunctionType

P = 128
PACK = 4
D, T, SLOTS, Q, E, M = 512, 1024, 512, 512, 512, 1024
BANK = 512
HALF = SLOTS // 2
LIST_ROWS = 16
FLOPS = 2 * D * Q * T + 2 * Q * E * SLOTS
S_SPLIT = 84


def tile_attend_difference_delivered_lean_kernel(tc, query, keys_words, keys_scales, qs, msgs, old, fade, offs, offs2, offs3, out):
    nc = tc.nc
    with ExitStack() as ctx:
        keep = ctx.enter_context(tc.tile_pool(name="keep", bufs=1))
        psum = ctx.enter_context(tc.psum_pool(name="psum", bufs=6))
        psum_keep = ctx.enter_context(tc.psum_pool(name="psum_keep", bufs=1))

        list1 = keep.tile([P, SLOTS // LIST_ROWS], U16, name="list1")
        list2 = keep.tile([P, SLOTS // LIST_ROWS], U16, name="list2")
        list3 = keep.tile([P, SLOTS // LIST_ROWS], U16, name="list3")
        q_raw = keep.tile([P, PACK, Q], F32, name="q_raw")
        m_raw = keep.tile([P, PACK, E], F32, name="m_raw")
        k_words = keep.tile([P, 2 * T], U8, name="k_words", align_bytes=64)
        k_scales = keep.tile([P, T], U8, name="k_scales", align_bytes=64)
        qs_cols = keep.tile([P, PACK], F32, name="qs_cols")
        fade_cols = keep.tile([P, M // BANK, PACK], F32, name="fade_cols")
        ident = keep.tile([P, P], F32, name="ident")
        fade_ps = [psum_keep.tile([P, PACK, P], F32, name="fade_ps%d" % b) for b in range(M // BANK)]
        old_sb = [keep.tile([P, M], F32, name="old%d" % e) for e in range(E // P)]
        placed = [keep.tile([P, M], F32, name="placed%d" % e) for e in range(E // P)]

        nc.sync.dma_start(out=q_raw[:], in_=query.rearrange("(p j) c -> p j c", j=PACK))
        nc.vector.memset(k_scales[:].bitcast(I32), 0)
        for quad in range(4):
            nc.scalar.dma_start(
                out=k_scales[32 * quad : 32 * quad + 4, :].bitcast(I32),
                in_=keys_scales[0, 4 * quad : 4 * quad + 4, :].bitcast(I32),
            )
        nc.sync.dma_start(out=k_words[:], in_=keys_words[0])
        nc.sync.dma_start(list2[:], offs2)
        nc.sync.dma_start(list1[:], offs)
        nc.sync.dma_start(out=m_raw[:], in_=msgs.rearrange("(p j) c -> p j c", j=PACK))
        nc.sync.dma_start(out=qs_cols[:], in_=qs.rearrange("(p j) o -> p (j o)", j=PACK))
        nc.sync.dma_start(out=fade_cols[:], in_=fade.rearrange("o (b p c) -> p (o b) c", p=P, c=PACK))
        nc.sync.dma_start(list3[:], offs3)
        for e in [1, 0, 3, 2]:
            nc.sync.dma_start(out=old_sb[e][:], in_=old[e * P : (e + 1) * P, :])
        make_identity(nc, ident[:])
        for e in range(E // P):
            nc.vector.memset(placed[e][:], 0.0)
        warm_in = keep.tile([P, 1], F32, name="warm_in")
        warm_out = keep.tile([P, 1], F32, name="warm_out")
        nc.vector.memset(warm_in[:], 0.0)
        nc.scalar.activation(warm_out[:], warm_in[:], ACT.Sigmoid)

        q_bf = keep.tile([P, PACK, P, PACK], BF16, name="q_bf", align_bytes=64)
        q_src = q_raw[:].rearrange("p j (s r) -> p s j r", r=PACK)
        q_dst = q_bf[:].rearrange("p r s j -> p s j r")
        nc.vector.tensor_copy(out=q_dst[:, :S_SPLIT], in_=q_src[:, :S_SPLIT])
        nc.scalar.activation(q_dst[:, S_SPLIT:], q_src[:, S_SPLIT:], ACT.Copy)
        q_codes = keep.tile([P, Q], U32, name="q_codes", align_bytes=64)
        q_scales = keep.tile([P, Q], U8, name="q_scales", align_bytes=64)
        a_sb = [keep.tile([P, T], F32, name="a%d" % r) for r in range(PACK)]
        for r in range(PACK):
            cols = slice(r * P, (r + 1) * P)
            nc.vector.quantize_mx(out=q_codes[:, cols].bitcast(FP8X4), scales=q_scales[:, cols], in_=q_bf[:, r].rearrange("p s j -> p (s j)"))

        m_bf = keep.tile([P, E, PACK], BF16, name="m_bf", align_bytes=64)
        m_codes = keep.tile([P, E], U32, name="m_codes", align_bytes=64)
        m_scales = keep.tile([P, E], U8, name="m_scales", align_bytes=64)
        second = [keep.tile([P, SLOTS], F32, name="second%d" % r) for r in range(PACK)]
        score = [keep.tile([P, SLOTS], F32, name="score%d" % r) for r in range(PACK)]
        weight = [keep.tile([P, SLOTS], F32, name="weight%d" % r) for r in range(PACK)]
        wq_rows = [keep.tile([P, PACK, HALF], BF16, name="wq_rows%d" % h) for h in range(2)]
        wq_bf = [keep.tile([P, HALF, PACK], BF16, name="wq_bf%d" % h, align_bytes=64) for h in range(2)]
        w_codes = [keep.tile([P, HALF], U32, name="w_codes%d" % h, align_bytes=64) for h in range(2)]
        w_scales = [keep.tile([P, HALF], U8, name="w_scales%d" % h, align_bytes=64) for h in range(2)]
        dl_sb = [keep.tile([P, SLOTS], F32, name="dl%d" % e) for e in range(E // P)]

        def copier(on_vector):
            return nc.vector.tensor_copy if on_vector else nc.scalar.copy

        def product(r, b, on_vector):
            cols = slice(r * P, (r + 1) * P)
            acc = psum.tile([P, BANK], F32, name="acc")
            nc.tensor.matmul_mx(
                out=acc[:],
                lhsT=q_codes[:, cols].bitcast(FP8X4),
                lhsT_scale=q_scales[:, cols],
                rhs=k_words[:, 2 * b * BANK : 2 * (b + 1) * BANK].bitcast(FP4X4),
                rhs_scale=k_scales[:, b * BANK : (b + 1) * BANK],
                start=True,
                stop=True,
            )
            copier(on_vector)(out=a_sb[r][:, b * BANK : (b + 1) * BANK], in_=acc[:])

        def spread_fade():
            for b in range(M // BANK):
                for c in range(PACK):
                    nc.tensor.transpose(fade_ps[b][:, c, :], fade_cols[:, b, c : c + 1].to_broadcast([P, P]), ident[:])

        def entries(lst, lo, hi):
            return lst[:, lo // LIST_ROWS : hi // LIST_ROWS]

        def gather2(r, lo, hi, on_vector=False):
            if on_vector:
                nc.vector.tensor_copy(second[r][:, lo:hi], a_sb[r][:].indirect(entries(list2, lo, hi)))
            else:
                nc.scalar.activation(second[r][:, lo:hi], a_sb[r][:].indirect(entries(list2, lo, hi)), ACT.Copy)

        def diff(r, lo, hi):
            nc.vector.tensor_tensor(score[r][:, lo:hi], a_sb[r][:].indirect(entries(list1, lo, hi)), second[r][:, lo:hi], ALU.subtract)

        def sig(r, lo, hi):
            nc.scalar.activation(weight[r][:, lo:hi], score[r][:, lo:hi], ACT.Sigmoid)

        def scale(r, h):
            nc.vector.tensor_scalar(wq_rows[h][:, r, :], weight[r][:, h * HALF : (h + 1) * HALF], qs_cols[:, r : r + 1], None, ALU.mult)

        def weave(h, on_vector):
            copier(on_vector)(
                out=wq_bf[h][:].rearrange("p (c i) r -> p c r i", i=4),
                in_=wq_rows[h][:].rearrange("p r (c i) -> p c r i", i=4),
            )

        def quant_w(h):
            nc.vector.quantize_mx(out=w_codes[h][:].bitcast(FP8X4), scales=w_scales[h][:], in_=wq_bf[h][:].rearrange("p i r -> p (i r)"))

        def msgs_cast(lo, hi, on_vector):
            copier(on_vector)(
                out=m_bf[:, lo:hi, :].rearrange("p (c i) j -> p c j i", i=4),
                in_=m_raw[:, :, lo:hi].rearrange("p j (c i) -> p c j i", i=4),
            )

        def msgs_quant(lo, hi):
            nc.vector.quantize_mx(out=m_codes[:, lo:hi].bitcast(FP8X4), scales=m_scales[:, lo:hi], in_=m_bf[:, lo:hi, :].rearrange("p c j -> p (c j)"))

        def deliver(e, h, on_vector):
            cols = slice(e * P, (e + 1) * P)
            acc = psum.tile([P, HALF], F32, name="acc")
            nc.tensor.matmul_mx(
                out=acc[:],
                lhsT=m_codes[:, cols].bitcast(FP8X4),
                lhsT_scale=m_scales[:, cols],
                rhs=w_codes[h][:].bitcast(FP8X4),
                rhs_scale=w_scales[h][:],
                start=True,
                stop=True,
            )
            copier(on_vector)(out=dl_sb[e][:, h * HALF : (h + 1) * HALF], in_=acc[:])

        def scatter(e, lo, hi, on_vector):
            if on_vector:
                nc.vector.tensor_copy(placed[e][:].indirect(entries(list3, lo, hi)), dl_sb[e][:, lo:hi])
            else:
                nc.scalar.activation(placed[e][:].indirect(entries(list3, lo, hi)), dl_sb[e][:, lo:hi], ACT.Copy)

        def fading(e):
            for b in range(2):
                view = old_sb[e][:, b * BANK : (b + 1) * BANK].rearrange("p (s c) -> p s c", c=PACK)
                nc.vector.tensor_tensor(view, view, fade_ps[b][:].rearrange("p c s -> p s c"), ALU.mult)

        def finish(e, b, eng):
            cols = slice(b * BANK, (b + 1) * BANK)
            eng.tensor_tensor(old_sb[e][:, cols], old_sb[e][:, cols], placed[e][:, cols], ALU.add)
            nc.sync.dma_start(out=out[e * P : (e + 1) * P, cols], in_=old_sb[e][:, cols])

        for r in range(PACK):
            product(r, 0, True)
            product(r, 1, False)
        spread_fade()
        for r in range(PACK - 1):
            gather2(r, 0, SLOTS)
            diff(r, 0, SLOTS)
        for h in range(2):
            gather2(3, h * HALF, (h + 1) * HALF)
            diff(3, h * HALF, (h + 1) * HALF)
        for r in range(PACK - 1):
            sig(r, 0, SLOTS)
        for h in range(2):
            sig(3, h * HALF, (h + 1) * HALF)
        msgs_cast(0, 256, True)
        msgs_quant(0, 256)
        for h in range(2):
            for r in range(PACK):
                scale(r, h)
        weave(0, True)
        weave(1, False)
        quant_w(0)
        quant_w(1)
        deliver(1, 0, False)
        deliver(0, 0, True)
        deliver(1, 1, False)
        deliver(0, 1, True)
        fading(1)
        msgs_cast(256, 512, True)
        msgs_quant(256, 512)
        scatter(1, 0, HALF, False)
        scatter(1, HALF, SLOTS, False)
        scatter(0, 0, SLOTS, True)
        finish(1, 0, nc.gpsimd)
        finish(1, 1, nc.gpsimd)
        fading(0)
        finish(0, 0, nc.gpsimd)
        finish(0, 1, nc.gpsimd)
        for h in range(2):
            deliver(3, h, False)
            scatter(3, h * HALF, (h + 1) * HALF, False)
        deliver(2, 0, True)
        scatter(2, 0, 128, True)
        deliver(2, 1, False)
        scatter(2, 128, SLOTS, False)
        fading(3)
        finish(3, 0, nc.vector)
        finish(3, 1, nc.vector)
        fading(2)
        finish(2, 0, nc.vector)
        finish(2, 1, nc.vector)
